import numpy as np
import ml_dtypes


def mxq(x, axis, fmt="e4m3"):
    dtype, down = {"e4m3": (ml_dtypes.float8_e4m3fn, 7), "e5m2": (ml_dtypes.float8_e5m2, 14)}[fmt]
    v = np.moveaxis(np.asarray(x, np.float32).astype(ml_dtypes.bfloat16).astype(np.float64), axis, -1)
    blocks = v.reshape(v.shape[:-1] + (-1, 32))
    amax = np.abs(blocks).max(-1, keepdims=True)
    byte = np.maximum(np.where(amax > 0, np.frexp(amax)[1] - 1 + 127, 0) - down, 1)
    scale = np.exp2(byte - 127.0)
    codes = (blocks / scale).astype(np.float32).astype(dtype).astype(np.float64)
    return np.moveaxis((codes * scale).reshape(v.shape), -1, axis)


WIDE = False


def mx_kscale(k):
    if not WIDE:
        return np.ones(k)
    levels = np.array([10, -10, 5, -5, 0])
    if k % 512:
        return np.exp2(np.random.permutation(np.resize(levels, k // 32))).repeat(32)
    a = np.empty((k // 512, 16))
    for p in range(k // 512):
        a[p, :8] = np.random.permutation(np.resize(levels, 8))
        for g in range(8):
            far = levels[np.abs(levels - a[p, g]) >= 10]
            a[p, g + 8] = far[np.random.randint(len(far))]
    return np.exp2(a.ravel()).repeat(32)


def f64(x):
    return np.asarray(x).astype(np.float64)


def striped(idx):
    return np.tile(idx.reshape(-1, 16).T, (8, 1)).astype(np.uint16)


def unstriped(offs):
    return offs[:16].T.reshape(-1).astype(np.int64)


def striped8(idx):
    return np.concatenate([x.reshape(-1, 16).T for x in idx]).astype(np.uint16)


def runs(offs, k):
    lists = np.stack([offs[16 * r : 16 * r + 16].T.reshape(-1) for r in range(8)]).astype(np.int64)
    return lists[np.arange(k) % 512 // 64]


def pack_weight(w):
    k, n = w.shape
    w = f64(np.asarray(w, np.float32).astype(ml_dtypes.bfloat16)).reshape(k // 32, 32, n)
    amax = np.abs(w).max(1)
    byte = np.clip(np.where(amax > 0, np.frexp(amax)[1] - 1 + 127 - 7, 1), 1, 254)
    scaled = (w * np.exp2(127.0 - byte)[:, None, :]).reshape(k, n).astype(np.float32)
    words = np.ascontiguousarray(scaled.reshape(k // 512, 128, 4, n).transpose(0, 1, 3, 2)).astype(ml_dtypes.float8_e4m3fn).view(np.uint8)
    return words, np.ascontiguousarray(byte.astype(np.uint8).reshape(k // 512, 16, n))


def unpack_weight(words, scales):
    g, p, n, _ = words.shape
    vals = np.ascontiguousarray(words).view(ml_dtypes.float8_e4m3fn).astype(np.float64) * np.repeat(np.exp2(scales.astype(np.float64) - 127.0), 8, axis=1)[..., None]
    return vals.transpose(0, 1, 3, 2).reshape(g * 512, n)


def relu(v):
    return np.maximum(v, 0.0)


def sigmoid(v):
    return 1.0 / (1.0 + np.exp(-np.maximum(v, -700.0)))


K, T, S, N, H = 512, 2048, 512, 512, 512


def setup_inputs():
    n = np.random.standard_normal
    s = mx_kscale(K)[:, None]
    u = mx_kscale(S)
    packed_xT = pack_weight(n((K, T)) * s)
    return {
        "x_words": packed_xT[0],
        "x_scales": packed_xT[1],
        "wa": (n((K, H)) / np.sqrt(K) / s).astype(np.float32),
        "gt": (np.random.uniform(0.5, 1.5, (S, 1)) * u[:, None]).astype(np.float32),
        "w1": (n((S, N)) / np.sqrt(S) / u[:, None]).astype(np.float32),
        "offs": striped(np.random.permutation(T)[:S]),
        "fo": striped8(np.stack([np.random.permutation(H) for _ in range(8)])),
    }


def reference(x_words, x_scales, wa, gt, w1, offs, fo):
    xq = unpack_weight(x_words, x_scales)[:, unstriped(offs)]
    y = xq.T @ mxq(f64(wa), 0, "e4m3")
    z = f64(gt) * relu(y)
    h = mxq(f64(w1), 0, "e4m3").T @ mxq(z, 0, "e4m3")
    return h * (sigmoid(h[np.arange(N)[:, None], runs(fo, N)]))

@@ -1,0 +1,173 @@
+from contextlib import ExitStack
+
+import concourse.mybir as mybir
+
+K, T, S, N, H = 512, 2048, 512, 512, 512
+FLOPS = 2 * S * K * H + 2 * N * S * H
+
+F32 = mybir.dt.float32
+BF16 = mybir.dt.bfloat16
+I32 = mybir.dt.int32
+U32 = mybir.dt.uint32
+U16 = mybir.dt.uint16
+U8 = mybir.dt.uint8
+FP8X4 = mybir.dt.float8_e4m3fn_x4
+ALU = mybir.AluOpType
+ACT = mybir.ActivationFunctionType
+
+P = 128
+PACK = 4
+CHUNK = 128
+HALF = 256
+
+
+def tile_picked_mixpick_none_p_kernel(tc, x_words, x_scales, wa, gt, w1, offs, fo, out):
+    nc = tc.nc
+    with ExitStack() as ctx:
+        pool = ctx.enter_context(tc.tile_pool(name="pool", bufs=1))
+        psum = ctx.enter_context(tc.psum_pool(name="psum", bufs=1))
+
+        offs_sb = pool.tile([P, S // 16], U16, name="offs_sb")
+        fo_sb = pool.tile([P, H // 16], U16, name="fo_sb")
+        xw = pool.tile([P, T], U32, name="xw", align_bytes=64)
+        xs = pool.tile([P, T], U8, name="xs", align_bytes=64)
+        gt_sb = pool.tile([P, PACK], F32, name="gt_sb")
+        warm = pool.tile([P, 8], F32, name="warm")
+        wa_raw = [pool.tile([P, PACK, HALF], F32, name=f"wa_raw{i}") for i in range(2)]
+        w1_raw = [pool.tile([P, PACK, HALF], F32, name=f"w1_raw{i}") for i in range(2)]
+
+        nc.vector.memset(xs[:].bitcast(I32), 0)
+        nc.vector.memset(warm[:, 0:1], 0.0)
+        nc.sync.dma_start(offs_sb[:], offs)
+        nc.sync.dma_start(out=xw[:].bitcast(I32), in_=x_words[0].rearrange("p n t -> p (n t)").bitcast(I32))
+        for q in range(4):
+            nc.scalar.dma_start(out=xs[32 * q : 32 * q + 4, :].bitcast(I32), in_=x_scales[0, 4 * q : 4 * q + 4, :].bitcast(I32))
+        nc.scalar.activation(out=warm[:, 1:2], in_=warm[:, 0:1], func=ACT.Sigmoid)
+        wa_rows = wa.rearrange("(p j) c -> p j c", j=PACK)
+        w1_rows = w1.rearrange("(p j) c -> p j c", j=PACK)
+        for i in range(2):
+            nc.sync.dma_start(out=wa_raw[i][:], in_=wa_rows[:, :, i * HALF : (i + 1) * HALF])
+        nc.sync.dma_start(out=gt_sb[:], in_=gt.rearrange("(p t) o -> p (t o)", t=PACK))
+        for i in range(2):
+            nc.sync.dma_start(out=w1_raw[i][:], in_=w1_rows[:, :, i * HALF : (i + 1) * HALF])
+        nc.sync.dma_start(fo_sb[:], fo)
+
+        xs_list = pool.tile([P, S], U8, name="xs_list", align_bytes=64)
+        xs_pick = pool.tile([P, S], U8, name="xs_pick", align_bytes=64)
+        xw_pick = pool.tile([P, S], U32, name="xw_pick", align_bytes=64)
+        nc.vector.tensor_copy(xs_list[:], xs[:].indirect(offs_sb[:]))
+        nc.vector.tensor_copy(out=xs_pick[:].rearrange("p (t m) -> p t m", t=PACK), in_=xs_list[:].rearrange("p (m t) -> p t m", t=PACK))
+        nc.vector.tensor_copy(xw_pick[:].rearrange("p (t m) -> p m t", t=PACK), xw[:].indirect(offs_sb[:]))
+
+        wa_codes = pool.tile([P, H], U32, name="wa_codes", align_bytes=64)
+        wa_scales = pool.tile([P, H], U8, name="wa_scales", align_bytes=64)
+        z_codes = pool.tile([P, H], U32, name="z_codes", align_bytes=64)
+        z_scales = pool.tile([P, H], U8, name="z_scales", align_bytes=64)
+        w1_codes = pool.tile([P, N], U32, name="w1_codes", align_bytes=64)
+        w1_scales = pool.tile([P, N], U8, name="w1_scales", align_bytes=64)
+        wa_bf = [pool.tile([P, CHUNK * PACK], BF16, name=f"wa_bf{c}", align_bytes=64) for c in range(4)]
+        z_bf = [pool.tile([P, CHUNK * PACK], BF16, name=f"z_bf{c}", align_bytes=64) for c in range(4)]
+        w1_bf = pool.tile([P, N * PACK], BF16, name="w1_bf", align_bytes=64)
+        y_ps = [psum.tile([P, PACK, CHUNK], F32, name=f"y_ps{c}") for c in range(4)]
+        h_ps = [psum.tile([P, H], F32, name=f"h_ps{t}") for t in range(PACK)]
+
+        def cols(c):
+            return slice(c * CHUNK, (c + 1) * CHUNK)
+
+        def weave_wa(c):
+            src = wa_raw[c // 2][:, :, (c % 2) * CHUNK : (c % 2 + 1) * CHUNK].rearrange("p j (a i) -> p a j i", i=4)
+            dst = wa_bf[c][:].rearrange("p (a i j) -> p a j i", i=4, j=PACK)
+            if c % 2 == 0:
+                nc.scalar.copy(out=dst, in_=src)
+            else:
+                nc.vector.tensor_copy(out=dst, in_=src)
+
+        def quant_wa(c):
+            nc.vector.quantize_mx(out=wa_codes[:, cols(c)].bitcast(FP8X4), scales=wa_scales[:, cols(c)], in_=wa_bf[c][:])
+
+        def project(c):
+            for t in range(PACK):
+                nc.tensor.matmul_mx(
+                    out=y_ps[c][:, t, :],
+                    lhsT=xw_pick[:, cols(t)].bitcast(FP8X4),
+                    lhsT_scale=xs_pick[:, cols(t)],
+                    rhs=wa_codes[:, cols(c)].bitcast(FP8X4),
+                    rhs_scale=wa_scales[:, cols(c)],
+                    start=True,
+                    stop=True,
+                )
+
+        def make_z(c):
+            nc.vector.scalar_tensor_tensor(
+                out=z_bf[c][:].rearrange("p (n t) -> p n t", t=PACK),
+                in0=y_ps[c][:].rearrange("p t n -> p n t"),
+                scalar=0.0,
+                in1=gt_sb[:].unsqueeze(1).to_broadcast([P, CHUNK, PACK]),
+                op0=ALU.max,
+                op1=ALU.mult,
+            )
+
+        def quant_z(c):
+            nc.vector.quantize_mx(out=z_codes[:, cols(c)].bitcast(FP8X4), scales=z_scales[:, cols(c)], in_=z_bf[c][:])
+
+        def weave_w1(i):
+            src = w1_raw[i][:].rearrange("p j (m t) -> p m j t", t=PACK)
+            dst = w1_bf[:].rearrange("p (t m j) -> p m j t", t=PACK, j=PACK)[:, i * 64 : (i + 1) * 64]
+            nc.scalar.copy(out=dst, in_=src)
+
+        def quant_w1(t):
+            nc.vector.quantize_mx(
+                out=w1_codes[:, cols(t)].bitcast(FP8X4), scales=w1_scales[:, cols(t)], in_=w1_bf[:, t * N : (t + 1) * N]
+            )
+
+        weave_wa(0)
+        weave_wa(1)
+        quant_wa(0)
+        quant_wa(1)
+        project(0)
+        project(1)
+        weave_wa(2)
+        weave_wa(3)
+        make_z(0)
+        quant_wa(2)
+        quant_wa(3)
+        project(2)
+        project(3)
+        weave_w1(0)
+        weave_w1(1)
+        make_z(1)
+        quant_z(0)
+        make_z(2)
+        quant_z(1)
+        make_z(3)
+        quant_z(2)
+        quant_w1(0)
+        quant_z(3)
+        for t in range(1, PACK):
+            quant_w1(t)
+
+        out_rows = out.rearrange("(p t) n -> p t n", t=PACK)
+        h_sb = [pool.tile([P, H], F32, name=f"h_sb{t}") for t in range(PACK)]
+        gate = [pool.tile([P, H], F32, name=f"gate{t}") for t in range(PACK)]
+        res = [pool.tile([P, H], F32, name=f"res{t}") for t in range(PACK)]
+        for t in range(PACK):
+            nc.tensor.matmul_mx(
+                out=h_ps[t][:],
+                lhsT=w1_codes[:, cols(t)].bitcast(FP8X4),
+                lhsT_scale=w1_scales[:, cols(t)],
+                rhs=z_codes[:].bitcast(FP8X4),
+                rhs_scale=z_scales[:],
+                start=True,
+                stop=True,
+            )
+        for t in range(PACK):
+            nc.vector.tensor_copy(out=h_sb[t][:], in_=h_ps[t][:])
+            for i in range(2):
+                nc.scalar.activation(
+                    out=gate[t][:, i * HALF : (i + 1) * HALF], in_=h_sb[t][:].indirect(fo_sb[:, i * 16 : (i + 1) * 16]), func=ACT.Sigmoid
+                )
+        for t in range(PACK):
+            for i in range(2):
+                half = slice(i * HALF, (i + 1) * HALF)
+                nc.vector.tensor_tensor(out=res[t][:, half], in0=h_ps[t][:, half], in1=gate[t][:, half], op=ALU.mult)
+            nc.sync.dma_start(out=out_rows[:, t, :], in_=res[t][:])

@@ -48,15 +48,15 @@ def tile_picked_mixpick_none_p_kernel(tc, x_words, x_scales, wa, gt, w1, offs, f
         for i in range(2):
             nc.sync.dma_start(out=wa_raw[i][:], in_=wa_rows[:, :, i * HALF : (i + 1) * HALF])
         nc.sync.dma_start(out=gt_sb[:], in_=gt.rearrange("(p t) o -> p (t o)", t=PACK))
+        nc.sync.dma_start(fo_sb[:], fo)
         for i in range(2):
             nc.sync.dma_start(out=w1_raw[i][:], in_=w1_rows[:, :, i * HALF : (i + 1) * HALF])
-        nc.sync.dma_start(fo_sb[:], fo)
 
-        xs_list = pool.tile([P, S], U8, name="xs_list", align_bytes=64)
+        xs_list = pool.tile([P, S], U8, name="xs_list", tag="picked", align_bytes=64)
         xs_pick = pool.tile([P, S], U8, name="xs_pick", align_bytes=64)
-        xw_pick = pool.tile([P, S], U32, name="xw_pick", align_bytes=64)
         nc.vector.tensor_copy(xs_list[:], xs[:].indirect(offs_sb[:]))
         nc.vector.tensor_copy(out=xs_pick[:].rearrange("p (t m) -> p t m", t=PACK), in_=xs_list[:].rearrange("p (m t) -> p t m", t=PACK))
+        xw_pick = pool.tile([P, S], U32, name="xw_pick", tag="picked", align_bytes=64)
         nc.vector.tensor_copy(xw_pick[:].rearrange("p (t m) -> p m t", t=PACK), xw[:].indirect(offs_sb[:]))
 
         wa_codes = pool.tile([P, H], U32, name="wa_codes", align_bytes=64)
@@ -68,8 +68,7 @@ def tile_picked_mixpick_none_p_kernel(tc, x_words, x_scales, wa, gt, w1, offs, f
         wa_bf = [pool.tile([P, CHUNK * PACK], BF16, name=f"wa_bf{c}", align_bytes=64) for c in range(4)]
         z_bf = [pool.tile([P, CHUNK * PACK], BF16, name=f"z_bf{c}", align_bytes=64) for c in range(4)]
         w1_bf = pool.tile([P, N * PACK], BF16, name="w1_bf", align_bytes=64)
-        y_ps = [psum.tile([P, PACK, CHUNK], F32, name=f"y_ps{c}") for c in range(4)]
-        h_ps = [psum.tile([P, H], F32, name=f"h_ps{t}") for t in range(PACK)]
+        y_ps = [psum.tile([P, PACK, CHUNK], F32, name=f"y_ps{c}", tag=f"bank{c}") for c in range(4)]
 
         def cols(c):
             return slice(c * CHUNK, (c + 1) * CHUNK)
@@ -77,7 +76,7 @@ def tile_picked_mixpick_none_p_kernel(tc, x_words, x_scales, wa, gt, w1, offs, f
         def weave_wa(c):
             src = wa_raw[c // 2][:, :, (c % 2) * CHUNK : (c % 2 + 1) * CHUNK].rearrange("p j (a i) -> p a j i", i=4)
             dst = wa_bf[c][:].rearrange("p (a i j) -> p a j i", i=4, j=PACK)
-            if c % 2 == 0:
+            if c != 1:
                 nc.scalar.copy(out=dst, in_=src)
             else:
                 nc.vector.tensor_copy(out=dst, in_=src)
@@ -122,23 +121,23 @@ def tile_picked_mixpick_none_p_kernel(tc, x_words, x_scales, wa, gt, w1, offs, f
 
         weave_wa(0)
         weave_wa(1)
-        quant_wa(0)
         quant_wa(1)
-        project(0)
+        quant_wa(0)
         project(1)
+        project(0)
         weave_wa(2)
         weave_wa(3)
-        make_z(0)
-        quant_wa(2)
-        quant_wa(3)
-        project(2)
-        project(3)
         weave_w1(0)
         weave_w1(1)
         make_z(1)
-        quant_z(0)
-        make_z(2)
+        quant_wa(2)
+        project(2)
+        make_z(0)
+        quant_wa(3)
+        project(3)
         quant_z(1)
+        make_z(2)
+        quant_z(0)
         make_z(3)
         quant_z(2)
         quant_w1(0)
@@ -150,24 +149,54 @@ def tile_picked_mixpick_none_p_kernel(tc, x_words, x_scales, wa, gt, w1, offs, f
         h_sb = [pool.tile([P, H], F32, name=f"h_sb{t}") for t in range(PACK)]
         gate = [pool.tile([P, H], F32, name=f"gate{t}") for t in range(PACK)]
         res = [pool.tile([P, H], F32, name=f"res{t}") for t in range(PACK)]
-        for t in range(PACK):
+        halves = [slice(0, HALF), slice(HALF, H)]
+        lists = [fo_sb[:, 0:16], fo_sb[:, 16:32]]
+
+        def mix(t, bank, c):
             nc.tensor.matmul_mx(
-                out=h_ps[t][:],
+                out=bank,
                 lhsT=w1_codes[:, cols(t)].bitcast(FP8X4),
                 lhsT_scale=w1_scales[:, cols(t)],
-                rhs=z_codes[:].bitcast(FP8X4),
-                rhs_scale=z_scales[:],
+                rhs=z_codes[:, c].bitcast(FP8X4),
+                rhs_scale=z_scales[:, c],
                 start=True,
                 stop=True,
             )
-        for t in range(PACK):
-            nc.vector.tensor_copy(out=h_sb[t][:], in_=h_ps[t][:])
+
+        h0 = [psum.tile([P, HALF], F32, name=f"h0_{i}") for i in range(2)]
+        h_ps = [None] + [psum.tile([P, H], F32, name=f"h_ps{t}", tag=f"bank{t - 1}") for t in range(1, PACK)]
+        for i in range(2):
+            mix(0, h0[i][:], halves[i])
+        for t in range(1, PACK):
+            mix(t, h_ps[t][:], slice(0, H))
+        nc.scalar.activation(out=gate[0][:, halves[0]], in_=h0[0][:], func=ACT.Sigmoid)
+        nc.vector.tensor_copy(out=h_sb[0][:, halves[1]], in_=h0[1][:])
+        nc.scalar.activation(out=gate[0][:, halves[1]], in_=h0[1][:], func=ACT.Sigmoid)
+        nc.vector.tensor_copy(out=h_sb[0][:, halves[0]], in_=h0[0][:])
+
+        def gate_then_gather(t):
             for i in range(2):
-                nc.scalar.activation(
-                    out=gate[t][:, i * HALF : (i + 1) * HALF], in_=h_sb[t][:].indirect(fo_sb[:, i * 16 : (i + 1) * 16]), func=ACT.Sigmoid
-                )
-        for t in range(PACK):
-            for i in range(2):
-                half = slice(i * HALF, (i + 1) * HALF)
-                nc.vector.tensor_tensor(out=res[t][:, half], in0=h_ps[t][:, half], in1=gate[t][:, half], op=ALU.mult)
+                nc.vector.tensor_tensor(out=res[t][:, halves[i]], in0=gate[t][:].indirect(lists[i]), in1=h_sb[t][:, halves[i]], op=ALU.mult)
             nc.sync.dma_start(out=out_rows[:, t, :], in_=res[t][:])
+
+        def gather_then_gate(t):
+            for i in range(2):
+                nc.scalar.activation(out=gate[t][:, halves[i]], in_=h_sb[t][:].indirect(lists[i]), func=ACT.Sigmoid)
+
+        def product(t, i):
+            nc.vector.tensor_tensor(out=res[t][:, halves[i]], in0=h_ps[t][:, halves[i]], in1=gate[t][:, halves[i]], op=ALU.mult)
+
+        nc.scalar.activation(out=gate[1][:], in_=h_ps[1][:], func=ACT.Sigmoid)
+        nc.scalar.copy(out=h_sb[1][:], in_=h_ps[1][:])
+        nc.scalar.copy(out=h_sb[2][:], in_=h_ps[2][:])
+        gate_then_gather(0)
+        nc.vector.tensor_copy(out=h_sb[3][:], in_=h_ps[3][:])
+        gather_then_gate(2)
+        gate_then_gather(1)
+        gather_then_gate(3)
+        product(2, 0)
+        product(2, 1)
+        nc.sync.dma_start(out=out_rows[:, 2, :], in_=res[2][:])
+        for i in range(2):
+            product(3, i)
+            nc.sync.dma_start(out=out_rows[:, 3, halves[i]], in_=res[3][:, halves[i]])

@@ -39,34 +39,33 @@ def tile_picked_mixpick_none_p_kernel(tc, x_words, x_scales, wa, gt, w1, offs, f
         nc.vector.memset(xs[:].bitcast(I32), 0)
         nc.vector.memset(warm[:, 0:1], 0.0)
         nc.sync.dma_start(offs_sb[:], offs)
-        nc.sync.dma_start(out=xw[:].bitcast(I32), in_=x_words[0].rearrange("p n t -> p (n t)").bitcast(I32))
-        for q in range(4):
-            nc.scalar.dma_start(out=xs[32 * q : 32 * q + 4, :].bitcast(I32), in_=x_scales[0, 4 * q : 4 * q + 4, :].bitcast(I32))
-        nc.scalar.activation(out=warm[:, 1:2], in_=warm[:, 0:1], func=ACT.Sigmoid)
         wa_rows = wa.rearrange("(p j) c -> p j c", j=PACK)
         w1_rows = w1.rearrange("(p j) c -> p j c", j=PACK)
-        for i in range(2):
-            nc.sync.dma_start(out=wa_raw[i][:], in_=wa_rows[:, :, i * HALF : (i + 1) * HALF])
+        nc.sync.dma_start(out=wa_raw[0][:], in_=wa_rows[:, :, 0:HALF])
+        for q in range(4):
+            nc.sync.dma_start(out=xs[32 * q : 32 * q + 4, :].bitcast(I32), in_=x_scales[0, 4 * q : 4 * q + 4, :].bitcast(I32))
+        nc.sync.dma_start(out=xw[:].bitcast(I32), in_=x_words[0].rearrange("p n t -> p (n t)").bitcast(I32))
+        nc.sync.dma_start(out=wa_raw[1][:], in_=wa_rows[:, :, HALF:H])
         nc.sync.dma_start(out=gt_sb[:], in_=gt.rearrange("(p t) o -> p (t o)", t=PACK))
         nc.sync.dma_start(fo_sb[:], fo)
         for i in range(2):
             nc.sync.dma_start(out=w1_raw[i][:], in_=w1_rows[:, :, i * HALF : (i + 1) * HALF])
+        nc.scalar.activation(out=warm[:, 1:2], in_=warm[:, 0:1], func=ACT.Sigmoid)
 
-        xs_list = pool.tile([P, S], U8, name="xs_list", tag="picked", align_bytes=64)
+        xs_list = pool.tile([P, S], U8, name="xs_list", tag="scale_bytes", align_bytes=64)
         xs_pick = pool.tile([P, S], U8, name="xs_pick", align_bytes=64)
+        xw_pick = pool.tile([P, S], U32, name="xw_pick", align_bytes=64)
         nc.vector.tensor_copy(xs_list[:], xs[:].indirect(offs_sb[:]))
         nc.vector.tensor_copy(out=xs_pick[:].rearrange("p (t m) -> p t m", t=PACK), in_=xs_list[:].rearrange("p (m t) -> p t m", t=PACK))
-        xw_pick = pool.tile([P, S], U32, name="xw_pick", tag="picked", align_bytes=64)
         nc.vector.tensor_copy(xw_pick[:].rearrange("p (t m) -> p m t", t=PACK), xw[:].indirect(offs_sb[:]))
 
         wa_codes = pool.tile([P, H], U32, name="wa_codes", align_bytes=64)
-        wa_scales = pool.tile([P, H], U8, name="wa_scales", align_bytes=64)
+        wa_scales = pool.tile([P, H], U8, name="wa_scales", tag="scale_bytes", align_bytes=64)
         z_codes = pool.tile([P, H], U32, name="z_codes", align_bytes=64)
         z_scales = pool.tile([P, H], U8, name="z_scales", align_bytes=64)
         w1_codes = pool.tile([P, N], U32, name="w1_codes", align_bytes=64)
         w1_scales = pool.tile([P, N], U8, name="w1_scales", align_bytes=64)
-        wa_bf = [pool.tile([P, CHUNK * PACK], BF16, name=f"wa_bf{c}", align_bytes=64) for c in range(4)]
-        z_bf = [pool.tile([P, CHUNK * PACK], BF16, name=f"z_bf{c}", align_bytes=64) for c in range(4)]
+        wa_bf = [pool.tile([P, CHUNK * PACK], BF16, name=f"wa_bf{c}", tag=f"woven{c}", align_bytes=64) for c in range(4)]
         w1_bf = pool.tile([P, N * PACK], BF16, name="w1_bf", align_bytes=64)
         y_ps = [psum.tile([P, PACK, CHUNK], F32, name=f"y_ps{c}", tag=f"bank{c}") for c in range(4)]
 
@@ -76,7 +75,7 @@ def tile_picked_mixpick_none_p_kernel(tc, x_words, x_scales, wa, gt, w1, offs, f
         def weave_wa(c):
             src = wa_raw[c // 2][:, :, (c % 2) * CHUNK : (c % 2 + 1) * CHUNK].rearrange("p j (a i) -> p a j i", i=4)
             dst = wa_bf[c][:].rearrange("p (a i j) -> p a j i", i=4, j=PACK)
-            if c != 1:
+            if c != 3:
                 nc.scalar.copy(out=dst, in_=src)
             else:
                 nc.vector.tensor_copy(out=dst, in_=src)
@@ -121,23 +120,24 @@ def tile_picked_mixpick_none_p_kernel(tc, x_words, x_scales, wa, gt, w1, offs, f
 
         weave_wa(0)
         weave_wa(1)
-        quant_wa(1)
         quant_wa(0)
-        project(1)
+        quant_wa(1)
         project(0)
+        project(1)
         weave_wa(2)
         weave_wa(3)
+        quant_wa(2)
+        quant_wa(3)
+        project(2)
+        project(3)
         weave_w1(0)
         weave_w1(1)
-        make_z(1)
-        quant_wa(2)
-        project(2)
+        z_bf = [pool.tile([P, CHUNK * PACK], BF16, name=f"z_bf{c}", tag=f"woven{PACK - 1 - c}", align_bytes=64) for c in range(4)]
         make_z(0)
-        quant_wa(3)
-        project(3)
-        quant_z(1)
-        make_z(2)
+        make_z(1)
         quant_z(0)
+        make_z(2)
+        quant_z(1)
         make_z(3)
         quant_z(2)
         quant_w1(0)
@@ -194,8 +194,7 @@ def tile_picked_mixpick_none_p_kernel(tc, x_words, x_scales, wa, gt, w1, offs, f
         gather_then_gate(2)
         gate_then_gather(1)
         gather_then_gate(3)
-        product(2, 0)
-        product(2, 1)
+        nc.vector.tensor_tensor(out=res[2][:], in0=h_ps[2][:], in1=gate[2][:], op=ALU.mult)
         nc.sync.dma_start(out=out_rows[:, 2, :], in_=res[2][:])
         for i in range(2):
             product(3, i)

@@ -17,8 +17,20 @@ ACT = mybir.ActivationFunctionType
 
 P = 128
 PACK = 4
+QUADRANT = 32
+GROUP = 16
+LINE = 4
 CHUNK = 128
+CHUNKS = H // CHUNK
 HALF = 256
+
+
+def chunk(c):
+    return slice(c * CHUNK, (c + 1) * CHUNK)
+
+
+def half(i):
+    return slice(i * HALF, (i + 1) * HALF)
 
 
 def tile_picked_mixpick_none_p_kernel(tc, x_words, x_scales, wa, gt, w1, offs, fo, out):
@@ -27,37 +39,39 @@ def tile_picked_mixpick_none_p_kernel(tc, x_words, x_scales, wa, gt, w1, offs, f
         pool = ctx.enter_context(tc.tile_pool(name="pool", bufs=1))
         psum = ctx.enter_context(tc.psum_pool(name="psum", bufs=1))
 
-        offs_sb = pool.tile([P, S // 16], U16, name="offs_sb")
-        fo_sb = pool.tile([P, H // 16], U16, name="fo_sb")
+        offs_sb = pool.tile([P, S // GROUP], U16, name="offs_sb")
+        fo_sb = pool.tile([P, H // GROUP], U16, name="fo_sb")
         xw = pool.tile([P, T], U32, name="xw", align_bytes=64)
         xs = pool.tile([P, T], U8, name="xs", align_bytes=64)
         gt_sb = pool.tile([P, PACK], F32, name="gt_sb")
-        warm = pool.tile([P, 8], F32, name="warm")
         wa_raw = [pool.tile([P, PACK, HALF], F32, name=f"wa_raw{i}") for i in range(2)]
         w1_raw = [pool.tile([P, PACK, HALF], F32, name=f"w1_raw{i}") for i in range(2)]
 
         nc.vector.memset(xs[:].bitcast(I32), 0)
-        nc.vector.memset(warm[:, 0:1], 0.0)
         nc.sync.dma_start(offs_sb[:], offs)
-        wa_rows = wa.rearrange("(p j) c -> p j c", j=PACK)
-        w1_rows = w1.rearrange("(p j) c -> p j c", j=PACK)
-        nc.sync.dma_start(out=wa_raw[0][:], in_=wa_rows[:, :, 0:HALF])
-        for q in range(4):
-            nc.sync.dma_start(out=xs[32 * q : 32 * q + 4, :].bitcast(I32), in_=x_scales[0, 4 * q : 4 * q + 4, :].bitcast(I32))
-        nc.sync.dma_start(out=xw[:].bitcast(I32), in_=x_words[0].rearrange("p n t -> p (n t)").bitcast(I32))
-        nc.sync.dma_start(out=wa_raw[1][:], in_=wa_rows[:, :, HALF:H])
-        nc.sync.dma_start(out=gt_sb[:], in_=gt.rearrange("(p t) o -> p (t o)", t=PACK))
+        wa_rows = wa.rearrange("(p r) c -> p r c", r=PACK)
+        w1_rows = w1.rearrange("(p r) c -> p r c", r=PACK)
+        nc.sync.dma_start(out=wa_raw[0][:], in_=wa_rows[:, :, half(0)])
+        for q in range(P // QUADRANT):
+            nc.sync.dma_start(
+                out=xs[QUADRANT * q : QUADRANT * q + PACK, :].bitcast(I32),
+                in_=x_scales[0, PACK * q : PACK * (q + 1), :].bitcast(I32),
+            )
+        nc.sync.dma_start(out=xw[:].bitcast(I32), in_=x_words[0].rearrange("p n r -> p (n r)").bitcast(I32))
+        nc.sync.dma_start(out=wa_raw[1][:], in_=wa_rows[:, :, half(1)])
+        nc.sync.dma_start(out=gt_sb[:], in_=gt.rearrange("(p r) o -> p (r o)", r=PACK))
         nc.sync.dma_start(fo_sb[:], fo)
         for i in range(2):
-            nc.sync.dma_start(out=w1_raw[i][:], in_=w1_rows[:, :, i * HALF : (i + 1) * HALF])
-        nc.scalar.activation(out=warm[:, 1:2], in_=warm[:, 0:1], func=ACT.Sigmoid)
+            nc.sync.dma_start(out=w1_raw[i][:], in_=w1_rows[:, :, half(i)])
 
         xs_list = pool.tile([P, S], U8, name="xs_list", tag="scale_bytes", align_bytes=64)
         xs_pick = pool.tile([P, S], U8, name="xs_pick", align_bytes=64)
         xw_pick = pool.tile([P, S], U32, name="xw_pick", align_bytes=64)
         nc.vector.tensor_copy(xs_list[:], xs[:].indirect(offs_sb[:]))
-        nc.vector.tensor_copy(out=xs_pick[:].rearrange("p (t m) -> p t m", t=PACK), in_=xs_list[:].rearrange("p (m t) -> p t m", t=PACK))
-        nc.vector.tensor_copy(xw_pick[:].rearrange("p (t m) -> p m t", t=PACK), xw[:].indirect(offs_sb[:]))
+        nc.vector.tensor_copy(
+            out=xs_pick[:].rearrange("p (r m) -> p r m", r=PACK), in_=xs_list[:].rearrange("p (m r) -> p r m", r=PACK)
+        )
+        nc.vector.tensor_copy(xw_pick[:].rearrange("p (r m) -> p m r", r=PACK), xw[:].indirect(offs_sb[:]))
 
         wa_codes = pool.tile([P, H], U32, name="wa_codes", align_bytes=64)
         wa_scales = pool.tile([P, H], U8, name="wa_scales", tag="scale_bytes", align_bytes=64)
@@ -65,137 +79,113 @@ def tile_picked_mixpick_none_p_kernel(tc, x_words, x_scales, wa, gt, w1, offs, f
         z_scales = pool.tile([P, H], U8, name="z_scales", align_bytes=64)
         w1_codes = pool.tile([P, N], U32, name="w1_codes", align_bytes=64)
         w1_scales = pool.tile([P, N], U8, name="w1_scales", align_bytes=64)
-        wa_bf = [pool.tile([P, CHUNK * PACK], BF16, name=f"wa_bf{c}", tag=f"woven{c}", align_bytes=64) for c in range(4)]
+        wa_bf = [pool.tile([P, CHUNK * PACK], BF16, name=f"wa_bf{c}", tag=f"woven{c}", align_bytes=64) for c in range(CHUNKS)]
         w1_bf = pool.tile([P, N * PACK], BF16, name="w1_bf", align_bytes=64)
-        y_ps = [psum.tile([P, PACK, CHUNK], F32, name=f"y_ps{c}", tag=f"bank{c}") for c in range(4)]
+        y_ps = [psum.tile([P, PACK, CHUNK], F32, name=f"y_ps{c}", tag=f"bank{c}") for c in range(CHUNKS)]
 
-        def cols(c):
-            return slice(c * CHUNK, (c + 1) * CHUNK)
+        def weave_wa(copy, c):
+            src = wa_raw[c // 2][:, :, chunk(c % 2)].rearrange("p r (a i) -> p a r i", i=LINE)
+            copy(out=wa_bf[c][:].rearrange("p (a i r) -> p a r i", i=LINE, r=PACK), in_=src)
 
-        def weave_wa(c):
-            src = wa_raw[c // 2][:, :, (c % 2) * CHUNK : (c % 2 + 1) * CHUNK].rearrange("p j (a i) -> p a j i", i=4)
-            dst = wa_bf[c][:].rearrange("p (a i j) -> p a j i", i=4, j=PACK)
-            if c != 3:
-                nc.scalar.copy(out=dst, in_=src)
-            else:
-                nc.vector.tensor_copy(out=dst, in_=src)
+        def weave_w1(i):
+            src = w1_raw[i][:].rearrange("p r (m t) -> p m r t", t=PACK)
+            dst = w1_bf[:].rearrange("p (t m r) -> p m r t", t=PACK, r=PACK)
+            nc.scalar.copy(out=dst[:, i * HALF // PACK : (i + 1) * HALF // PACK], in_=src)
 
-        def quant_wa(c):
-            nc.vector.quantize_mx(out=wa_codes[:, cols(c)].bitcast(FP8X4), scales=wa_scales[:, cols(c)], in_=wa_bf[c][:])
+        def quantize(codes, scales, columns, woven):
+            nc.vector.quantize_mx(out=codes[:, columns].bitcast(FP8X4), scales=scales[:, columns], in_=woven)
+
+        def product_mx(result, lhs_codes, lhs_scales, lhs_columns, rhs_codes, rhs_scales, rhs_columns):
+            nc.tensor.matmul_mx(
+                out=result,
+                lhsT=lhs_codes[:, lhs_columns].bitcast(FP8X4),
+                lhsT_scale=lhs_scales[:, lhs_columns],
+                rhs=rhs_codes[:, rhs_columns].bitcast(FP8X4),
+                rhs_scale=rhs_scales[:, rhs_columns],
+                start=True,
+                stop=True,
+            )
 
         def project(c):
-            for t in range(PACK):
-                nc.tensor.matmul_mx(
-                    out=y_ps[c][:, t, :],
-                    lhsT=xw_pick[:, cols(t)].bitcast(FP8X4),
-                    lhsT_scale=xs_pick[:, cols(t)],
-                    rhs=wa_codes[:, cols(c)].bitcast(FP8X4),
-                    rhs_scale=wa_scales[:, cols(c)],
-                    start=True,
-                    stop=True,
-                )
+            for r in range(PACK):
+                product_mx(y_ps[c][:, r, :], xw_pick, xs_pick, chunk(r), wa_codes, wa_scales, chunk(c))
+
+        for i in range(2):
+            pair = (2 * i, 2 * i + 1)
+            for c in pair:
+                weave_wa(nc.vector.tensor_copy if c == CHUNKS - 1 else nc.scalar.copy, c)
+            for c in pair:
+                quantize(wa_codes, wa_scales, chunk(c), wa_bf[c][:])
+            for c in pair:
+                project(c)
+        for i in range(2):
+            weave_w1(i)
+
+        z_bf = [
+            pool.tile([P, CHUNK * PACK], BF16, name=f"z_bf{c}", tag=f"woven{CHUNKS - 1 - c}", align_bytes=64)
+            for c in range(CHUNKS)
+        ]
 
         def make_z(c):
             nc.vector.scalar_tensor_tensor(
-                out=z_bf[c][:].rearrange("p (n t) -> p n t", t=PACK),
-                in0=y_ps[c][:].rearrange("p t n -> p n t"),
+                out=z_bf[c][:].rearrange("p (n r) -> p n r", r=PACK),
+                in0=y_ps[c][:].rearrange("p r n -> p n r"),
                 scalar=0.0,
                 in1=gt_sb[:].unsqueeze(1).to_broadcast([P, CHUNK, PACK]),
                 op0=ALU.max,
                 op1=ALU.mult,
             )
 
-        def quant_z(c):
-            nc.vector.quantize_mx(out=z_codes[:, cols(c)].bitcast(FP8X4), scales=z_scales[:, cols(c)], in_=z_bf[c][:])
+        def quantize_z(c):
+            quantize(z_codes, z_scales, chunk(c), z_bf[c][:])
 
-        def weave_w1(i):
-            src = w1_raw[i][:].rearrange("p j (m t) -> p m j t", t=PACK)
-            dst = w1_bf[:].rearrange("p (t m j) -> p m j t", t=PACK, j=PACK)[:, i * 64 : (i + 1) * 64]
-            nc.scalar.copy(out=dst, in_=src)
+        def quantize_w1(first, last):
+            columns = slice(first * CHUNK, last * CHUNK)
+            quantize(w1_codes, w1_scales, columns, w1_bf[:, first * CHUNK * PACK : last * CHUNK * PACK])
 
-        def quant_w1(t):
-            nc.vector.quantize_mx(
-                out=w1_codes[:, cols(t)].bitcast(FP8X4), scales=w1_scales[:, cols(t)], in_=w1_bf[:, t * N : (t + 1) * N]
-            )
-
-        weave_wa(0)
-        weave_wa(1)
-        quant_wa(0)
-        quant_wa(1)
-        project(0)
-        project(1)
-        weave_wa(2)
-        weave_wa(3)
-        quant_wa(2)
-        quant_wa(3)
-        project(2)
-        project(3)
-        weave_w1(0)
-        weave_w1(1)
-        z_bf = [pool.tile([P, CHUNK * PACK], BF16, name=f"z_bf{c}", tag=f"woven{PACK - 1 - c}", align_bytes=64) for c in range(4)]
         make_z(0)
-        make_z(1)
-        quant_z(0)
-        make_z(2)
-        quant_z(1)
-        make_z(3)
-        quant_z(2)
-        quant_w1(0)
-        quant_z(3)
+        for c in range(1, CHUNKS):
+            make_z(c)
+            quantize_z(c - 1)
+        quantize_w1(0, 1)
+        quantize_z(CHUNKS - 1)
+        quantize_w1(1, 2)
+        quantize_w1(2, PACK)
+
+        h_first = [psum.tile([P, HALF], F32, name=f"h_first{i}") for i in range(2)]
+        h_ps = {t: psum.tile([P, H], F32, name=f"h_ps{t}", tag=f"bank{t - 1}") for t in range(1, PACK)}
+        for i in range(2):
+            product_mx(h_first[i][:], w1_codes, w1_scales, chunk(0), z_codes, z_scales, half(i))
         for t in range(1, PACK):
-            quant_w1(t)
+            product_mx(h_ps[t][:], w1_codes, w1_scales, chunk(t), z_codes, z_scales, slice(0, H))
 
         out_rows = out.rearrange("(p t) n -> p t n", t=PACK)
-        h_sb = [pool.tile([P, H], F32, name=f"h_sb{t}") for t in range(PACK)]
+        rows = [pool.tile([P, H], F32, name=f"rows{t}") for t in range(PACK)]
         gate = [pool.tile([P, H], F32, name=f"gate{t}") for t in range(PACK)]
         res = [pool.tile([P, H], F32, name=f"res{t}") for t in range(PACK)]
-        halves = [slice(0, HALF), slice(HALF, H)]
-        lists = [fo_sb[:, 0:16], fo_sb[:, 16:32]]
+        lists = [fo_sb[:, i * HALF // GROUP : (i + 1) * HALF // GROUP] for i in range(2)]
 
-        def mix(t, bank, c):
-            nc.tensor.matmul_mx(
-                out=bank,
-                lhsT=w1_codes[:, cols(t)].bitcast(FP8X4),
-                lhsT_scale=w1_scales[:, cols(t)],
-                rhs=z_codes[:, c].bitcast(FP8X4),
-                rhs_scale=z_scales[:, c],
-                start=True,
-                stop=True,
-            )
+        def fetch_on_vector(t):
+            for i in range(2):
+                nc.vector.tensor_copy(out=gate[t][:, half(i)], in_=rows[t][:].indirect(lists[i]))
 
-        h0 = [psum.tile([P, HALF], F32, name=f"h0_{i}") for i in range(2)]
-        h_ps = [None] + [psum.tile([P, H], F32, name=f"h_ps{t}", tag=f"bank{t - 1}") for t in range(1, PACK)]
+        def apply_gate(t, i, h):
+            nc.vector.tensor_tensor(out=res[t][:, half(i)], in0=h, in1=gate[t][:, half(i)], op=ALU.mult)
+
         for i in range(2):
-            mix(0, h0[i][:], halves[i])
+            nc.scalar.activation(out=rows[0][:, half(i)], in_=h_first[i][:], func=ACT.Sigmoid)
+        nc.scalar.activation(out=rows[1][:], in_=h_ps[1][:], func=ACT.Sigmoid)
+        for t in range(2, PACK):
+            nc.scalar.copy(out=rows[t][:], in_=h_ps[t][:])
+            for i in range(2):
+                nc.scalar.activation(out=gate[t][:, half(i)], in_=rows[t][:].indirect(lists[i]), func=ACT.Sigmoid)
+
+        fetch_on_vector(0)
+        for i in range(2):
+            apply_gate(0, i, h_first[i][:])
+        nc.sync.dma_start(out=out_rows[:, 0, :], in_=res[0][:])
+        fetch_on_vector(1)
         for t in range(1, PACK):
-            mix(t, h_ps[t][:], slice(0, H))
-        nc.scalar.activation(out=gate[0][:, halves[0]], in_=h0[0][:], func=ACT.Sigmoid)
-        nc.vector.tensor_copy(out=h_sb[0][:, halves[1]], in_=h0[1][:])
-        nc.scalar.activation(out=gate[0][:, halves[1]], in_=h0[1][:], func=ACT.Sigmoid)
-        nc.vector.tensor_copy(out=h_sb[0][:, halves[0]], in_=h0[0][:])
-
-        def gate_then_gather(t):
             for i in range(2):
-                nc.vector.tensor_tensor(out=res[t][:, halves[i]], in0=gate[t][:].indirect(lists[i]), in1=h_sb[t][:, halves[i]], op=ALU.mult)
-            nc.sync.dma_start(out=out_rows[:, t, :], in_=res[t][:])
-
-        def gather_then_gate(t):
-            for i in range(2):
-                nc.scalar.activation(out=gate[t][:, halves[i]], in_=h_sb[t][:].indirect(lists[i]), func=ACT.Sigmoid)
-
-        def product(t, i):
-            nc.vector.tensor_tensor(out=res[t][:, halves[i]], in0=h_ps[t][:, halves[i]], in1=gate[t][:, halves[i]], op=ALU.mult)
-
-        nc.scalar.activation(out=gate[1][:], in_=h_ps[1][:], func=ACT.Sigmoid)
-        nc.scalar.copy(out=h_sb[1][:], in_=h_ps[1][:])
-        nc.scalar.copy(out=h_sb[2][:], in_=h_ps[2][:])
-        gate_then_gather(0)
-        nc.vector.tensor_copy(out=h_sb[3][:], in_=h_ps[3][:])
-        gather_then_gate(2)
-        gate_then_gather(1)
-        gather_then_gate(3)
-        nc.vector.tensor_tensor(out=res[2][:], in0=h_ps[2][:], in1=gate[2][:], op=ALU.mult)
-        nc.sync.dma_start(out=out_rows[:, 2, :], in_=res[2][:])
-        for i in range(2):
-            product(3, i)
-            nc.sync.dma_start(out=out_rows[:, 3, halves[i]], in_=res[3][:, halves[i]])
+                apply_gate(t, i, h_ps[t][:, half(i)])
+                nc.sync.dma_start(out=out_rows[:, t, half(i)], in_=res[t][:, half(i)])

from contextlib import ExitStack

import concourse.mybir as mybir

K, T, S, N, H = 512, 2048, 512, 512, 512
FLOPS = 2 * S * K * H + 2 * N * S * H

F32 = mybir.dt.float32
BF16 = mybir.dt.bfloat16
I32 = mybir.dt.int32
U32 = mybir.dt.uint32
U16 = mybir.dt.uint16
U8 = mybir.dt.uint8
FP8X4 = mybir.dt.float8_e4m3fn_x4
ALU = mybir.AluOpType
ACT = mybir.ActivationFunctionType

P = 128
PACK = 4
QUADRANT = 32
GROUP = 16
LINE = 4
CHUNK = 128
CHUNKS = H // CHUNK
HALF = 256


def chunk(c):
    return slice(c * CHUNK, (c + 1) * CHUNK)


def half(i):
    return slice(i * HALF, (i + 1) * HALF)


def tile_picked_mixpick_none_p_kernel(tc, x_words, x_scales, wa, gt, w1, offs, fo, out):
    nc = tc.nc
    with ExitStack() as ctx:
        pool = ctx.enter_context(tc.tile_pool(name="pool", bufs=1))
        psum = ctx.enter_context(tc.psum_pool(name="psum", bufs=1))

        offs_sb = pool.tile([P, S // GROUP], U16, name="offs_sb")
        fo_sb = pool.tile([P, H // GROUP], U16, name="fo_sb")
        xw = pool.tile([P, T], U32, name="xw", align_bytes=64)
        xs = pool.tile([P, T], U8, name="xs", align_bytes=64)
        gt_sb = pool.tile([P, PACK], F32, name="gt_sb")
        wa_raw = [pool.tile([P, PACK, HALF], F32, name=f"wa_raw{i}") for i in range(2)]
        w1_raw = [pool.tile([P, PACK, HALF], F32, name=f"w1_raw{i}") for i in range(2)]

        nc.vector.memset(xs[:].bitcast(I32), 0)
        nc.sync.dma_start(offs_sb[:], offs)
        wa_rows = wa.rearrange("(p r) c -> p r c", r=PACK)
        w1_rows = w1.rearrange("(p r) c -> p r c", r=PACK)
        nc.sync.dma_start(out=wa_raw[0][:], in_=wa_rows[:, :, half(0)])
        for q in range(P // QUADRANT):
            nc.sync.dma_start(
                out=xs[QUADRANT * q : QUADRANT * q + PACK, :].bitcast(I32),
                in_=x_scales[0, PACK * q : PACK * (q + 1), :].bitcast(I32),
            )
        nc.sync.dma_start(out=xw[:].bitcast(I32), in_=x_words[0].rearrange("p n r -> p (n r)").bitcast(I32))
        nc.sync.dma_start(out=wa_raw[1][:], in_=wa_rows[:, :, half(1)])
        nc.sync.dma_start(out=gt_sb[:], in_=gt.rearrange("(p r) o -> p (r o)", r=PACK))
        nc.sync.dma_start(fo_sb[:], fo)
        for i in range(2):
            nc.sync.dma_start(out=w1_raw[i][:], in_=w1_rows[:, :, half(i)])

        xs_list = pool.tile([P, S], U8, name="xs_list", tag="scale_bytes", align_bytes=64)
        xs_pick = pool.tile([P, S], U8, name="xs_pick", align_bytes=64)
        xw_pick = pool.tile([P, S], U32, name="xw_pick", align_bytes=64)
        nc.vector.tensor_copy(xs_list[:], xs[:].indirect(offs_sb[:]))
        nc.vector.tensor_copy(
            out=xs_pick[:].rearrange("p (r m) -> p r m", r=PACK), in_=xs_list[:].rearrange("p (m r) -> p r m", r=PACK)
        )
        nc.vector.tensor_copy(xw_pick[:].rearrange("p (r m) -> p m r", r=PACK), xw[:].indirect(offs_sb[:]))

        wa_codes = pool.tile([P, H], U32, name="wa_codes", align_bytes=64)
        wa_scales = pool.tile([P, H], U8, name="wa_scales", tag="scale_bytes", align_bytes=64)
        z_codes = pool.tile([P, H], U32, name="z_codes", align_bytes=64)
        z_scales = pool.tile([P, H], U8, name="z_scales", align_bytes=64)
        w1_codes = pool.tile([P, N], U32, name="w1_codes", align_bytes=64)
        w1_scales = pool.tile([P, N], U8, name="w1_scales", align_bytes=64)
        wa_bf = [pool.tile([P, CHUNK * PACK], BF16, name=f"wa_bf{c}", tag=f"woven{c}", align_bytes=64) for c in range(CHUNKS)]
        w1_bf = pool.tile([P, N * PACK], BF16, name="w1_bf", align_bytes=64)
        y_ps = [psum.tile([P, PACK, CHUNK], F32, name=f"y_ps{c}", tag=f"bank{c}") for c in range(CHUNKS)]

        def weave_wa(copy, c):
            src = wa_raw[c // 2][:, :, chunk(c % 2)].rearrange("p r (a i) -> p a r i", i=LINE)
            copy(out=wa_bf[c][:].rearrange("p (a i r) -> p a r i", i=LINE, r=PACK), in_=src)

        def weave_w1(i):
            src = w1_raw[i][:].rearrange("p r (m t) -> p m r t", t=PACK)
            dst = w1_bf[:].rearrange("p (t m r) -> p m r t", t=PACK, r=PACK)
            nc.scalar.copy(out=dst[:, i * HALF // PACK : (i + 1) * HALF // PACK], in_=src)

        def quantize(codes, scales, columns, woven):
            nc.vector.quantize_mx(out=codes[:, columns].bitcast(FP8X4), scales=scales[:, columns], in_=woven)

        def product_mx(result, lhs_codes, lhs_scales, lhs_columns, rhs_codes, rhs_scales, rhs_columns):
            nc.tensor.matmul_mx(
                out=result,
                lhsT=lhs_codes[:, lhs_columns].bitcast(FP8X4),
                lhsT_scale=lhs_scales[:, lhs_columns],
                rhs=rhs_codes[:, rhs_columns].bitcast(FP8X4),
                rhs_scale=rhs_scales[:, rhs_columns],
                start=True,
                stop=True,
            )

        def project(c):
            for r in range(PACK):
                product_mx(y_ps[c][:, r, :], xw_pick, xs_pick, chunk(r), wa_codes, wa_scales, chunk(c))

        for i in range(2):
            pair = (2 * i, 2 * i + 1)
            for c in pair:
                weave_wa(nc.vector.tensor_copy if c == CHUNKS - 1 else nc.scalar.copy, c)
            for c in pair:
                quantize(wa_codes, wa_scales, chunk(c), wa_bf[c][:])
            for c in pair:
                project(c)
        for i in range(2):
            weave_w1(i)

        z_bf = [
            pool.tile([P, CHUNK * PACK], BF16, name=f"z_bf{c}", tag=f"woven{CHUNKS - 1 - c}", align_bytes=64)
            for c in range(CHUNKS)
        ]

        def make_z(c):
            nc.vector.scalar_tensor_tensor(
                out=z_bf[c][:].rearrange("p (n r) -> p n r", r=PACK),
                in0=y_ps[c][:].rearrange("p r n -> p n r"),
                scalar=0.0,
                in1=gt_sb[:].unsqueeze(1).to_broadcast([P, CHUNK, PACK]),
                op0=ALU.max,
                op1=ALU.mult,
            )

        def quantize_z(c):
            quantize(z_codes, z_scales, chunk(c), z_bf[c][:])

        def quantize_w1(first, last):
            columns = slice(first * CHUNK, last * CHUNK)
            quantize(w1_codes, w1_scales, columns, w1_bf[:, first * CHUNK * PACK : last * CHUNK * PACK])

        make_z(0)
        for c in range(1, CHUNKS):
            make_z(c)
            quantize_z(c - 1)
        quantize_w1(0, 1)
        quantize_z(CHUNKS - 1)
        quantize_w1(1, 2)
        quantize_w1(2, PACK)

        h_first = [psum.tile([P, HALF], F32, name=f"h_first{i}") for i in range(2)]
        h_ps = {t: psum.tile([P, H], F32, name=f"h_ps{t}", tag=f"bank{t - 1}") for t in range(1, PACK)}
        for i in range(2):
            product_mx(h_first[i][:], w1_codes, w1_scales, chunk(0), z_codes, z_scales, half(i))
        for t in range(1, PACK):
            product_mx(h_ps[t][:], w1_codes, w1_scales, chunk(t), z_codes, z_scales, slice(0, H))

        out_rows = out.rearrange("(p t) n -> p t n", t=PACK)
        rows = [pool.tile([P, H], F32, name=f"rows{t}") for t in range(PACK)]
        gate = [pool.tile([P, H], F32, name=f"gate{t}") for t in range(PACK)]
        res = [pool.tile([P, H], F32, name=f"res{t}") for t in range(PACK)]
        lists = [fo_sb[:, i * HALF // GROUP : (i + 1) * HALF // GROUP] for i in range(2)]

        def fetch_on_vector(t):
            for i in range(2):
                nc.vector.tensor_copy(out=gate[t][:, half(i)], in_=rows[t][:].indirect(lists[i]))

        def apply_gate(t, i, h):
            nc.vector.tensor_tensor(out=res[t][:, half(i)], in0=h, in1=gate[t][:, half(i)], op=ALU.mult)

        for i in range(2):
            nc.scalar.activation(out=rows[0][:, half(i)], in_=h_first[i][:], func=ACT.Sigmoid)
        nc.scalar.activation(out=rows[1][:], in_=h_ps[1][:], func=ACT.Sigmoid)
        for t in range(2, PACK):
            nc.scalar.copy(out=rows[t][:], in_=h_ps[t][:])
            for i in range(2):
                nc.scalar.activation(out=gate[t][:, half(i)], in_=rows[t][:].indirect(lists[i]), func=ACT.Sigmoid)

        fetch_on_vector(0)
        for i in range(2):
            apply_gate(0, i, h_first[i][:])
        nc.sync.dma_start(out=out_rows[:, 0, :], in_=res[0][:])
        fetch_on_vector(1)
        for t in range(1, PACK):
            for i in range(2):
                apply_gate(t, i, h_ps[t][:, half(i)])
                nc.sync.dma_start(out=out_rows[:, t, half(i)], in_=res[t][:, half(i)])
